import numpy as np
import ml_dtypes


def mxq(x, axis, fmt="e4m3"):
    dtype, down = {"e4m3": (ml_dtypes.float8_e4m3fn, 7), "e5m2": (ml_dtypes.float8_e5m2, 14)}[fmt]
    v = np.moveaxis(np.asarray(x, np.float32).astype(ml_dtypes.bfloat16).astype(np.float64), axis, -1)
    blocks = v.reshape(v.shape[:-1] + (-1, 32))
    amax = np.abs(blocks).max(-1, keepdims=True)
    byte = np.maximum(np.where(amax > 0, np.frexp(amax)[1] - 1 + 127, 0) - down, 1)
    scale = np.exp2(byte - 127.0)
    codes = (blocks / scale).astype(np.float32).astype(dtype).astype(np.float64)
    return np.moveaxis((codes * scale).reshape(v.shape), -1, axis)


WIDE = False


def mx_kscale(k):
    if not WIDE:
        return np.ones(k)
    levels = np.array([24, -24, 12, -12, 0])
    if k % 512:
        return np.exp2(np.random.permutation(np.resize(levels, k // 32))).repeat(32)
    a = np.empty((k // 512, 16))
    for p in range(k // 512):
        a[p, :8] = np.random.permutation(np.resize(levels, 8))
        for g in range(8):
            far = levels[np.abs(levels - a[p, g]) >= 10]
            a[p, g + 8] = far[np.random.randint(len(far))]
    return np.exp2(a.ravel()).repeat(32)


def f64(x):
    return np.asarray(x).astype(np.float64)


def striped8(idx):
    return np.concatenate([v.reshape(-1, 16).T for v in idx]).astype(np.uint16)


def unstriped8(offs):
    return np.stack([offs[16 * g:16 * g + 16].T.reshape(-1) for g in range(8)]).astype(np.int64)


E2M1 = np.array([0.0, 0.5, 1.0, 1.5, 2.0, 3.0, 4.0, 6.0, -0.0, -0.5, -1.0, -1.5, -2.0, -3.0, -4.0, -6.0])


def pack_weight(w, fmt):
    k, n = w.shape
    w = f64(np.asarray(w, np.float32).astype(ml_dtypes.bfloat16)).reshape(k // 32, 32, n)
    amax = np.abs(w).max(1)
    if fmt == "e4m3":
        byte = np.frexp(amax)[1] - 1 + 127 - 7
    else:
        mant, ex = np.frexp(amax / 6.0)
        byte = np.where(mant > 0.5, ex, ex - 1) + 127
    byte = np.clip(np.where(amax > 0, byte, 1), 1, 254)
    scaled = (w * np.exp2(127.0 - byte)[:, None, :]).reshape(k, n).astype(np.float32)
    by_word = np.ascontiguousarray(scaled.reshape(k // 512, 128, 4, n).transpose(0, 1, 3, 2))
    if fmt == "e4m3":
        words = by_word.astype(ml_dtypes.float8_e4m3fn).view(np.uint8)
    else:
        c = by_word.astype(ml_dtypes.float4_e2m1fn).view(np.uint8) & 0xF
        words = (c[..., 0::2] | (c[..., 1::2] << 4)).reshape(k // 512, 128, 2 * n)
    return np.ascontiguousarray(words), np.ascontiguousarray(byte.astype(np.uint8).reshape(k // 512, 16, n))


def unpack_weight(words, scales, fmt):
    g, _, n = scales.shape
    words = np.ascontiguousarray(words).reshape(g, 128, n, -1)
    if fmt == "e4m3":
        vals = words.view(ml_dtypes.float8_e4m3fn).astype(np.float64)
    else:
        nib = np.empty((g, 128, n, 4), np.uint8)
        nib[..., 0::2] = words & 0xF
        nib[..., 1::2] = words >> 4
        vals = E2M1[nib]
    vals = vals * np.repeat(np.exp2(scales.astype(np.float64) - 127.0), 8, axis=1)[..., None]
    return vals.transpose(0, 1, 3, 2).reshape(g * 512, n)


def silu(f):
    return f / (1.0 + np.exp(-np.maximum(f, -700.0)))


K, L, N, T, J = 512, 512, 512, 2048, 1024


def setup_inputs():
    n = np.random.standard_normal
    s = mx_kscale(K)[:, None]
    s2 = mx_kscale(L)[:, None]
    p_wa = pack_weight(n((K, N)) / np.sqrt(K) / s, "e4m3")
    p_wb = pack_weight(n((L, N)) / np.sqrt(L) / s2, "e4m3")
    return {
        "xT": (n((K, T)) * s).astype(np.float32),
        "wgt": np.repeat(np.random.uniform(0.5, 2.0, (8, J)), 16, axis=0).astype(np.float32),
        "zT": (n((L, T)) * s2).astype(np.float32),
        "wgt2": np.repeat(np.random.uniform(0.5, 2.0, (8, J)), 16, axis=0).astype(np.float32),
        "wa_words": p_wa[0],
        "wa_scales": p_wa[1],
        "wb_words": p_wb[0],
        "wb_scales": p_wb[1],
        "b": (0.3 * n(N)).astype(np.float32),
        "offs": striped8(np.stack([np.random.permutation(T)[:J] for _ in range(8)])),
        "offs2": striped8(np.stack([np.random.permutation(T)[:J] for _ in range(8)])),
    }


def reference(xT, wgt, zT, wgt2, wa_words, wa_scales, wb_words, wb_scales, b, offs, offs2):
    idx = unstriped8(offs)
    idx2 = unstriped8(offs2)
    rows = np.arange(K)
    xg = f64(wgt)[rows // 4 % 128] * f64(xT)[rows[:, None], idx[rows % 512 // 64]]
    xT_ = mxq(xg, 0, "e4m3")
    rows = np.arange(L)
    xg = f64(wgt2)[rows // 4 % 128] * f64(zT)[rows[:, None], idx2[rows % 512 // 64]]
    zT_ = mxq(xg, 0, "e4m3")
    wa_ = unpack_weight(wa_words, wa_scales, "e4m3")
    wb_ = unpack_weight(wb_words, wb_scales, "e4m3")
    ya = wa_.T @ xT_
    yb = wb_.T @ zT_
    return silu(silu(ya) * yb + f64(b)[:, None])

@@ -1,0 +1,178 @@
+from contextlib import ExitStack
+
+import concourse.mybir as mybir
+
+K, N, T, J = 512, 512, 2048, 1024
+FLOPS = 2 * 2 * K * N * J
+
+F32 = mybir.dt.float32
+BF16 = mybir.dt.bfloat16
+I32 = mybir.dt.int32
+U32 = mybir.dt.uint32
+U16 = mybir.dt.uint16
+U8 = mybir.dt.uint8
+FP8X4 = mybir.dt.float8_e4m3fn_x4
+MULT = mybir.AluOpType.mult
+SILU = mybir.ActivationFunctionType.Silu
+
+P = 128
+PACK = 4
+LIST = 16
+M_TILES = N // P
+BANK = 512
+X_W = 512
+Z_W = 256
+
+
+def tile_list_glu_silu_kernel(
+    tc, xT, wgt, zT, wgt2, wa_words, wa_scales, wb_words, wb_scales, b, offs, offs2, out
+):
+    nc = tc.nc
+    with ExitStack() as ctx:
+        keep = ctx.enter_context(tc.tile_pool(name="keep", bufs=1))
+        psum = ctx.enter_context(tc.psum_pool(name="psum", bufs=8))
+
+        x_offs = keep.tile([P, J // LIST], U16, name="x_offs")
+        z_offs = keep.tile([P, J // LIST], U16, name="z_offs")
+        x_gain = keep.tile([P, J], F32, name="x_gain")
+        z_gain = keep.tile([P, J], F32, name="z_gain")
+        x_planes = [keep.tile([P, T], F32, name="x_plane%d" % i) for i in range(PACK)]
+        z_planes = [keep.tile([P, T], F32, name="z_plane%d" % i) for i in range(PACK)]
+        x_pairs = [keep.tile([P, 2, J], F32, name="x_pair%d" % u) for u in range(2)]
+        z_pairs = [keep.tile([P, 2, J], F32, name="z_pair%d" % u) for u in range(2)]
+        wa_codes = keep.tile([P, N], U32, name="wa_codes", align_bytes=64)
+        wb_codes = keep.tile([P, N], U32, name="wb_codes", align_bytes=64)
+        wa_plane = keep.tile([P, N], U8, name="wa_plane", align_bytes=64)
+        wb_plane = keep.tile([P, N], U8, name="wb_plane", align_bytes=64)
+        bias = keep.tile([P, M_TILES], F32, name="bias")
+        warm = keep.tile([P, 8], F32, name="warm")
+        warm_out = keep.tile([P, 8], F32, name="warm_out")
+
+        nc.vector.memset(warm[:], 0.0)
+        nc.scalar.activation(warm_out[:], warm[:], SILU)
+        nc.vector.memset(wa_plane[:].bitcast(I32), 0)
+        nc.vector.memset(wb_plane[:].bitcast(I32), 0)
+
+        x_rows = xT.rearrange("(p i) t -> p i t", i=PACK)
+        z_rows = zT.rearrange("(p i) t -> p i t", i=PACK)
+        out_rows = out.rearrange("(m p) j -> p m j", p=P)
+
+        def load_scales(plane, scales, q):
+            nc.sync.dma_start(plane[32 * q : 32 * q + 4, :].bitcast(I32), scales[0, 4 * q : 4 * q + 4, :].bitcast(I32))
+
+        def load_words(codes, words):
+            nc.sync.dma_start(codes[:].bitcast(I32), words[0].rearrange("p n i -> p (n i)").bitcast(I32))
+
+        half = J // 2
+        nc.sync.dma_start(x_offs[:], offs)
+        nc.sync.dma_start(x_gain[:, :half], wgt[:, :half])
+        nc.sync.dma_start(x_planes[0][:], x_rows[:, 0, :])
+        nc.sync.dma_start(x_gain[:, half:], wgt[:, half:])
+        nc.sync.dma_start(x_planes[1][:], x_rows[:, 1, :])
+        nc.sync.dma_start(z_offs[:], offs2)
+        load_scales(wa_plane, wa_scales, 0)
+        nc.sync.dma_start(x_planes[2][:], x_rows[:, 2, :])
+        load_scales(wa_plane, wa_scales, 1)
+        load_scales(wa_plane, wa_scales, 2)
+        nc.sync.dma_start(x_planes[3][:], x_rows[:, 3, :])
+        load_scales(wa_plane, wa_scales, 3)
+        nc.sync.dma_start(z_gain[:, :half], wgt2[:, :half])
+        nc.sync.dma_start(z_planes[0][:], z_rows[:, 0, :])
+        load_words(wa_codes, wa_words)
+        nc.sync.dma_start(z_gain[:, half:], wgt2[:, half:])
+        load_scales(wb_plane, wb_scales, 0)
+        nc.sync.dma_start(z_planes[1][:], z_rows[:, 1, :])
+        load_scales(wb_plane, wb_scales, 1)
+        load_scales(wb_plane, wb_scales, 2)
+        nc.sync.dma_start(z_planes[2][:], z_rows[:, 2, :])
+        load_scales(wb_plane, wb_scales, 3)
+        nc.sync.dma_start(z_planes[3][:], z_rows[:, 3, :])
+        load_words(wb_codes, wb_words)
+        with nc.allow_non_contiguous_dma(reason="one bias value for each partition and output tile"):
+            nc.sync.dma_start(bias[:], b.rearrange("(m p) -> p m", p=P))
+
+        def gather(pairs, planes, offsets, gain, i, j0, width):
+            picked = planes[i][:].indirect(offsets[:, j0 // LIST : (j0 + width) // LIST])
+            nc.vector.tensor_tensor(pairs[i // 2][:, i % 2, j0 : j0 + width], picked, gain[:, j0 : j0 + width], MULT)
+
+        def interleave(grouped, pairs, u, j0, width):
+            nc.scalar.copy(grouped[:, :, 2 * u : 2 * u + 2], pairs[u][:, :, j0 : j0 + width].rearrange("p e j -> p j e"))
+
+        def quantize(codes, plane, grouped):
+            nc.vector.quantize_mx(out=codes[:].bitcast(FP8X4), scales=plane[:], in_=grouped[:].rearrange("p j i -> p (j i)"))
+
+        def project(acc, w_codes, w_plane, m, codes, plane):
+            cols = slice(m * P, (m + 1) * P)
+            nc.tensor.matmul_mx(
+                out=acc,
+                lhsT=w_codes[:, cols].bitcast(FP8X4),
+                lhsT_scale=w_plane[:, cols],
+                rhs=codes[:].bitcast(FP8X4),
+                rhs_scale=plane[:],
+                start=True,
+                stop=True,
+            )
+
+        def stage_tiles(name, count, width):
+            grouped = [keep.tile([P, width, PACK], BF16, name="%s_grouped%d" % (name, s), align_bytes=64) for s in range(count)]
+            codes = [keep.tile([P, width], U32, name="%s_codes%d" % (name, s), align_bytes=64) for s in range(count)]
+            planes = [keep.tile([P, width], U8, name="%s_scales%d" % (name, s), align_bytes=64) for s in range(count)]
+            return grouped, codes, planes
+
+        x_slices, z_slices = J // X_W, J // Z_W
+        x_grouped, x_codes, x_scales = stage_tiles("x", x_slices, X_W)
+        z_grouped, z_codes, z_scales = stage_tiles("z", z_slices, Z_W)
+        gates = [keep.tile([P, M_TILES, X_W], F32, name="gate%d" % s) for s in range(x_slices)]
+
+        for i in range(PACK):
+            for s in range(x_slices):
+                gather(x_pairs, x_planes, x_offs, x_gain, i, s * X_W, X_W)
+                if i % 2 == 1:
+                    interleave(x_grouped[s], x_pairs, i // 2, s * X_W, X_W)
+        for s in range(x_slices):
+            quantize(x_codes[s], x_scales[s], x_grouped[s])
+            for m in range(M_TILES):
+                acc = psum.tile([P, BANK], F32, name="acc")
+                project(acc[:], wa_codes, wa_plane, m, x_codes[s], x_scales[s])
+                nc.scalar.activation(gates[s][:, m, :], acc[:], SILU)
+
+        for i in range(PACK - 1):
+            for h in range(2):
+                gather(z_pairs, z_planes, z_offs, z_gain, i, h * half, half)
+                if i == 1:
+                    for s in range(h * half // Z_W, (h + 1) * half // Z_W):
+                        interleave(z_grouped[s], z_pairs, 0, s * Z_W, Z_W)
+
+        per_bank = BANK // Z_W
+
+        def front(s):
+            gather(z_pairs, z_planes, z_offs, z_gain, PACK - 1, s * Z_W, Z_W)
+            interleave(z_grouped[s], z_pairs, 1, s * Z_W, Z_W)
+
+        def middle(s):
+            quantize(z_codes[s], z_scales[s], z_grouped[s])
+
+        def back(s):
+            j0 = s * Z_W
+            gate = gates[j0 // X_W]
+            g0 = j0 % X_W
+            for m0 in range(0, M_TILES, per_bank):
+                acc = psum.tile([P, BANK], F32, name="acc")
+                for m in range(per_bank):
+                    project(acc[:, m * Z_W : (m + 1) * Z_W], wb_codes, wb_plane, m0 + m, z_codes[s], z_scales[s])
+                product = keep.tile([P, per_bank, Z_W], F32, name="product%d_%d" % (s, m0))
+                result = keep.tile([P, per_bank, Z_W], F32, name="result%d_%d" % (s, m0))
+                nc.vector.tensor_tensor(
+                    product[:], acc[:].rearrange("p (m j) -> p m j", m=per_bank), gate[:, m0 : m0 + per_bank, g0 : g0 + Z_W], MULT
+                )
+                for m in range(per_bank):
+                    nc.scalar.activation(result[:, m, :], product[:, m, :], SILU, bias=bias[:, m0 + m : m0 + m + 1])
+                nc.sync.dma_start(out_rows[:, m0 : m0 + per_bank, j0 : j0 + Z_W], result[:])
+
+        for step in range(z_slices + 3):
+            if step < z_slices:
+                front(step)
+            if 0 <= step - 2 < z_slices:
+                middle(step - 2)
+            if 0 <= step - 3 < z_slices:
+                back(step - 3)

@@ -1,6 +1,7 @@
 from contextlib import ExitStack
 
 import concourse.mybir as mybir
+from concourse.masks import make_identity
 
 K, N, T, J = 512, 512, 2048, 1024
 FLOPS = 2 * 2 * K * N * J
@@ -18,10 +19,14 @@ SILU = mybir.ActivationFunctionType.Silu
 P = 128
 PACK = 4
 LIST = 16
+HEADS = P // LIST
+CHUNKS = J // P
 M_TILES = N // P
 BANK = 512
-X_W = 512
-Z_W = 256
+W = 256
+SLICES = J // W
+HALF = J // 2
+PER_BANK = BANK // W
 
 
 def tile_list_glu_silu_kernel(
@@ -30,149 +35,198 @@ def tile_list_glu_silu_kernel(
     nc = tc.nc
     with ExitStack() as ctx:
         keep = ctx.enter_context(tc.tile_pool(name="keep", bufs=1))
+        ring = ctx.enter_context(tc.tile_pool(name="ring", bufs=2))
         psum = ctx.enter_context(tc.psum_pool(name="psum", bufs=8))
 
         x_offs = keep.tile([P, J // LIST], U16, name="x_offs")
         z_offs = keep.tile([P, J // LIST], U16, name="z_offs")
         x_gain = keep.tile([P, J], F32, name="x_gain")
         z_gain = keep.tile([P, J], F32, name="z_gain")
-        x_planes = [keep.tile([P, T], F32, name="x_plane%d" % i) for i in range(PACK)]
-        z_planes = [keep.tile([P, T], F32, name="z_plane%d" % i) for i in range(PACK)]
-        x_pairs = [keep.tile([P, 2, J], F32, name="x_pair%d" % u) for u in range(2)]
-        z_pairs = [keep.tile([P, 2, J], F32, name="z_pair%d" % u) for u in range(2)]
+        x_quad = keep.tile([P, PACK, J], F32, name="x_quad")
+        z_quad = keep.tile([P, PACK, J], F32, name="z_quad")
         wa_codes = keep.tile([P, N], U32, name="wa_codes", align_bytes=64)
-        wb_codes = keep.tile([P, N], U32, name="wb_codes", align_bytes=64)
         wa_plane = keep.tile([P, N], U8, name="wa_plane", align_bytes=64)
         wb_plane = keep.tile([P, N], U8, name="wb_plane", align_bytes=64)
-        bias = keep.tile([P, M_TILES], F32, name="bias")
+        gain_rows = keep.tile([P, P], F32, name="gain_rows")
+        identity = keep.tile([P, P], F32, name="identity")
         warm = keep.tile([P, 8], F32, name="warm")
         warm_out = keep.tile([P, 8], F32, name="warm_out")
+        gates = [keep.tile([P, M_TILES, W], F32, name="gate%d" % s) for s in range(SLICES)]
 
+        def stage_tiles(name):
+            grouped = [keep.tile([P, W, PACK], BF16, name="%s_grouped%d" % (name, s), align_bytes=64) for s in range(SLICES)]
+            codes = [keep.tile([P, W], U32, name="%s_codes%d" % (name, s), align_bytes=64) for s in range(SLICES)]
+            planes = [keep.tile([P, W], U8, name="%s_scales%d" % (name, s), align_bytes=64) for s in range(SLICES)]
+            return grouped, codes, planes
+
+        x_grouped, x_codes, x_scales = stage_tiles("x")
+        z_grouped, z_codes, z_scales = stage_tiles("z")
+
+        make_identity(nc, identity[:])
         nc.vector.memset(warm[:], 0.0)
         nc.scalar.activation(warm_out[:], warm[:], SILU)
         nc.vector.memset(wa_plane[:].bitcast(I32), 0)
         nc.vector.memset(wb_plane[:].bitcast(I32), 0)
 
-        x_rows = xT.rearrange("(p i) t -> p i t", i=PACK)
-        z_rows = zT.rearrange("(p i) t -> p i t", i=PACK)
         out_rows = out.rearrange("(m p) j -> p m j", p=P)
 
-        def load_scales(plane, scales, q):
-            nc.sync.dma_start(plane[32 * q : 32 * q + 4, :].bitcast(I32), scales[0, 4 * q : 4 * q + 4, :].bitcast(I32))
+        def load_window(source, i):
+            window = keep.tile([P, T], F32, name="window%d" % i)
+            nc.sync.dma_start(window[:], source.rearrange("(p i) t -> p i t", i=PACK)[:, i, :])
+            return window
+
+        def load_scales(plane, scales):
+            for q in range(4):
+                nc.sync.dma_start(plane[32 * q : 32 * q + 4, :].bitcast(I32), scales[0, 4 * q : 4 * q + 4, :].bitcast(I32))
 
         def load_words(codes, words):
             nc.sync.dma_start(codes[:].bitcast(I32), words[0].rearrange("p n i -> p (n i)").bitcast(I32))
 
-        half = J // 2
-        nc.sync.dma_start(x_offs[:], offs)
-        nc.sync.dma_start(x_gain[:, :half], wgt[:, :half])
-        nc.sync.dma_start(x_planes[0][:], x_rows[:, 0, :])
-        nc.sync.dma_start(x_gain[:, half:], wgt[:, half:])
-        nc.sync.dma_start(x_planes[1][:], x_rows[:, 1, :])
-        nc.sync.dma_start(z_offs[:], offs2)
-        load_scales(wa_plane, wa_scales, 0)
-        nc.sync.dma_start(x_planes[2][:], x_rows[:, 2, :])
-        load_scales(wa_plane, wa_scales, 1)
-        load_scales(wa_plane, wa_scales, 2)
-        nc.sync.dma_start(x_planes[3][:], x_rows[:, 3, :])
-        load_scales(wa_plane, wa_scales, 3)
-        nc.sync.dma_start(z_gain[:, :half], wgt2[:, :half])
-        nc.sync.dma_start(z_planes[0][:], z_rows[:, 0, :])
-        load_words(wa_codes, wa_words)
-        nc.sync.dma_start(z_gain[:, half:], wgt2[:, half:])
-        load_scales(wb_plane, wb_scales, 0)
-        nc.sync.dma_start(z_planes[1][:], z_rows[:, 1, :])
-        load_scales(wb_plane, wb_scales, 1)
-        load_scales(wb_plane, wb_scales, 2)
-        nc.sync.dma_start(z_planes[2][:], z_rows[:, 2, :])
-        load_scales(wb_plane, wb_scales, 3)
-        nc.sync.dma_start(z_planes[3][:], z_rows[:, 3, :])
-        load_words(wb_codes, wb_words)
-        with nc.allow_non_contiguous_dma(reason="one bias value for each partition and output tile"):
-            nc.sync.dma_start(bias[:], b.rearrange("(m p) -> p m", p=P))
+        def gather(target, window, offsets, gain, j0, width):
+            picked = window[:].indirect(offsets[:, j0 // LIST : (j0 + width) // LIST])
+            nc.vector.tensor_tensor(target, picked, gain[:, j0 : j0 + width], MULT)
 
-        def gather(pairs, planes, offsets, gain, i, j0, width):
-            picked = planes[i][:].indirect(offsets[:, j0 // LIST : (j0 + width) // LIST])
-            nc.vector.tensor_tensor(pairs[i // 2][:, i % 2, j0 : j0 + width], picked, gain[:, j0 : j0 + width], MULT)
+        def interleave_pair(grouped, u, pair):
+            nc.scalar.copy(grouped[:, :, 2 * u : 2 * u + 2], pair.rearrange("p e j -> p j e"))
 
-        def interleave(grouped, pairs, u, j0, width):
-            nc.scalar.copy(grouped[:, :, 2 * u : 2 * u + 2], pairs[u][:, :, j0 : j0 + width].rearrange("p e j -> p j e"))
+        def interleave_all(grouped, quad):
+            nc.scalar.copy(
+                grouped[:].rearrange("p (c r) i -> p c i r", r=4),
+                quad.rearrange("p i (c r) -> p c i r", r=4),
+            )
 
         def quantize(codes, plane, grouped):
             nc.vector.quantize_mx(out=codes[:].bitcast(FP8X4), scales=plane[:], in_=grouped[:].rearrange("p j i -> p (j i)"))
 
-        def project(acc, w_codes, w_plane, m, codes, plane):
-            cols = slice(m * P, (m + 1) * P)
-            nc.tensor.matmul_mx(
-                out=acc,
-                lhsT=w_codes[:, cols].bitcast(FP8X4),
-                lhsT_scale=w_plane[:, cols],
-                rhs=codes[:].bitcast(FP8X4),
-                rhs_scale=plane[:],
-                start=True,
-                stop=True,
-            )
-
-        def stage_tiles(name, count, width):
-            grouped = [keep.tile([P, width, PACK], BF16, name="%s_grouped%d" % (name, s), align_bytes=64) for s in range(count)]
-            codes = [keep.tile([P, width], U32, name="%s_codes%d" % (name, s), align_bytes=64) for s in range(count)]
-            planes = [keep.tile([P, width], U8, name="%s_scales%d" % (name, s), align_bytes=64) for s in range(count)]
-            return grouped, codes, planes
-
-        x_slices, z_slices = J // X_W, J // Z_W
-        x_grouped, x_codes, x_scales = stage_tiles("x", x_slices, X_W)
-        z_grouped, z_codes, z_scales = stage_tiles("z", z_slices, Z_W)
-        gates = [keep.tile([P, M_TILES, X_W], F32, name="gate%d" % s) for s in range(x_slices)]
-
-        for i in range(PACK):
-            for s in range(x_slices):
-                gather(x_pairs, x_planes, x_offs, x_gain, i, s * X_W, X_W)
-                if i % 2 == 1:
-                    interleave(x_grouped[s], x_pairs, i // 2, s * X_W, X_W)
-        for s in range(x_slices):
-            quantize(x_codes[s], x_scales[s], x_grouped[s])
-            for m in range(M_TILES):
-                acc = psum.tile([P, BANK], F32, name="acc")
-                project(acc[:], wa_codes, wa_plane, m, x_codes[s], x_scales[s])
-                nc.scalar.activation(gates[s][:, m, :], acc[:], SILU)
-
-        for i in range(PACK - 1):
-            for h in range(2):
-                gather(z_pairs, z_planes, z_offs, z_gain, i, h * half, half)
-                if i == 1:
-                    for s in range(h * half // Z_W, (h + 1) * half // Z_W):
-                        interleave(z_grouped[s], z_pairs, 0, s * Z_W, Z_W)
-
-        per_bank = BANK // Z_W
-
-        def front(s):
-            gather(z_pairs, z_planes, z_offs, z_gain, PACK - 1, s * Z_W, Z_W)
-            interleave(z_grouped[s], z_pairs, 1, s * Z_W, Z_W)
-
-        def middle(s):
-            quantize(z_codes[s], z_scales[s], z_grouped[s])
-
-        def back(s):
-            j0 = s * Z_W
-            gate = gates[j0 // X_W]
-            g0 = j0 % X_W
-            for m0 in range(0, M_TILES, per_bank):
-                acc = psum.tile([P, BANK], F32, name="acc")
-                for m in range(per_bank):
-                    project(acc[:, m * Z_W : (m + 1) * Z_W], wb_codes, wb_plane, m0 + m, z_codes[s], z_scales[s])
-                product = keep.tile([P, per_bank, Z_W], F32, name="product%d_%d" % (s, m0))
-                result = keep.tile([P, per_bank, Z_W], F32, name="result%d_%d" % (s, m0))
-                nc.vector.tensor_tensor(
-                    product[:], acc[:].rearrange("p (m j) -> p m j", m=per_bank), gate[:, m0 : m0 + per_bank, g0 : g0 + Z_W], MULT
+        def project_bank(w_codes, w_plane, m0, codes, plane):
+            acc = psum.tile([P, PER_BANK, W], F32, name="acc")
+            for m in range(PER_BANK):
+                cols = slice((m0 + m) * P, (m0 + m + 1) * P)
+                nc.tensor.matmul_mx(
+                    out=acc[:, m, :],
+                    lhsT=w_codes[:, cols].bitcast(FP8X4),
+                    lhsT_scale=w_plane[:, cols],
+                    rhs=codes[:].bitcast(FP8X4),
+                    rhs_scale=plane[:],
+                    start=True,
+                    stop=True,
                 )
-                for m in range(per_bank):
-                    nc.scalar.activation(result[:, m, :], product[:, m, :], SILU, bias=bias[:, m0 + m : m0 + m + 1])
-                nc.sync.dma_start(out_rows[:, m0 : m0 + per_bank, j0 : j0 + Z_W], result[:])
+            return acc
 
-        for step in range(z_slices + 3):
-            if step < z_slices:
-                front(step)
-            if 0 <= step - 2 < z_slices:
-                middle(step - 2)
-            if 0 <= step - 3 < z_slices:
-                back(step - 3)
+        for stream, gain_in in enumerate((wgt, wgt2)):
+            nc.sync.dma_start(
+                gain_rows[64 * stream : 64 * (stream + 1), :],
+                gain_in.rearrange("(g r) (c j) -> r g c j", r=LIST, j=P)[0],
+            )
+        nc.sync.dma_start(x_offs[:], offs)
+        nc.sync.dma_start(x_gain[:, :W], wgt[:, :W])
+        x_windows = [load_window(xT, 0), load_window(xT, 1)]
+        nc.sync.dma_start(z_offs[:], offs2)
+        x_windows.append(load_window(xT, 2))
+        load_scales(wa_plane, wa_scales)
+        x_windows.append(load_window(xT, 3))
+        load_words(wa_codes, wa_words)
+        load_scales(wb_plane, wb_scales)
+
+        turned = psum.tile([P, P], F32, name="acc")
+        nc.tensor.transpose(turned[:], gain_rows[:], identity[:])
+        turned_view = turned[:].rearrange("p (s g c) -> p s c g", s=2, g=HEADS)
+
+        def spread_gain(gain, stream, c0, count):
+            spread = ring.tile([P, count, P], F32, name="spread")
+            nc.scalar.copy(
+                spread[:].rearrange("p c (g r) -> p c g r", r=LIST),
+                turned_view[:, stream, c0 : c0 + count, :].unsqueeze(3).to_broadcast([P, count, HEADS, LIST]),
+            )
+            back_turned = psum.tile([P, count, P], F32, name="acc")
+            for c in range(count):
+                nc.tensor.transpose(back_turned[:, c, :], spread[:, c, :], identity[:])
+            nc.scalar.copy(gain[:, c0 * P : (c0 + count) * P].rearrange("p (c j) -> p c j", j=P), back_turned[:])
+
+        spread_gain(x_gain, 0, 2, 2)
+        spread_gain(x_gain, 0, 4, 4)
+        spread_gain(z_gain, 1, 0, 4)
+        spread_gain(z_gain, 1, 4, 4)
+
+        def cols(s):
+            return slice(s * W, (s + 1) * W)
+
+        def gather_x(i, j0, width):
+            gather(x_quad[:, i, j0 : j0 + width], x_windows[i], x_offs, x_gain, j0, width)
+
+        for j0, width in ((0, W), (W, W), (HALF, HALF)):
+            gather_x(0, j0, width)
+        for h in range(2):
+            gather_x(1, h * HALF, HALF)
+            for s in (2 * h, 2 * h + 1):
+                interleave_pair(x_grouped[s], 0, x_quad[:, 0:2, cols(s)])
+        for h in range(2):
+            gather_x(2, h * HALF, HALF)
+        for s in range(SLICES):
+            gather_x(3, s * W, W)
+            interleave_pair(x_grouped[s], 1, x_quad[:, 2:4, cols(s)])
+
+        z_windows = [load_window(zT, i) for i in range(PACK)]
+
+        for s in range(SLICES):
+            quantize(x_codes[s], x_scales[s], x_grouped[s])
+            for m0 in range(0, M_TILES, PER_BANK):
+                acc = project_bank(wa_codes, wa_plane, m0, x_codes[s], x_scales[s])
+                nc.scalar.activation(gates[s][:, m0 : m0 + PER_BANK, :], acc[:], SILU)
+
+        wb_codes = keep.tile([P, N], U32, name="x_grouped3", align_bytes=64)
+        load_words(wb_codes, wb_words)
+        bias = keep.tile([P, M_TILES], F32, name="x_codes3", align_bytes=64)
+        with nc.allow_non_contiguous_dma(reason="one bias value for each partition and output tile"):
+            nc.sync.dma_start(bias[:], b.rearrange("(m p) -> p m", p=P))
+
+        def gather_z(i, j0, width):
+            gather(z_quad[:, i, j0 : j0 + width], z_windows[i], z_offs, z_gain, j0, width)
+
+        for h in range(2):
+            gather_z(0, h * HALF, HALF)
+        for h in range(2):
+            gather_z(1, h * HALF, HALF)
+        for s in (0, 1, 3):
+            interleave_pair(z_grouped[s], 0, z_quad[:, 0:2, cols(s)])
+        gather_z(2, 0, 3 * W)
+
+        def finish(s, m0, count):
+            acc = banks[(s, m0 - m0 % PER_BANK)]
+            a0 = m0 % PER_BANK
+            product = keep.tile([P, count, W], F32, name="product%d_%d" % (s, m0))
+            result = keep.tile([P, count, W], F32, name="result%d_%d" % (s, m0))
+            nc.vector.tensor_tensor(product[:], acc[:, a0 : a0 + count, :], gates[s][:, m0 : m0 + count, :], MULT)
+            for m in range(count):
+                nc.scalar.activation(result[:, m, :], product[:, m, :], SILU, bias=bias[:, m0 + m : m0 + m + 1])
+            nc.sync.dma_start(out_rows[:, m0 : m0 + count, cols(s)], result[:])
+
+        banks = {}
+
+        def project_z(s):
+            quantize(z_codes[s], z_scales[s], z_grouped[s])
+            for m0 in range(0, M_TILES, PER_BANK):
+                banks.setdefault((s, m0), project_bank(wb_codes, wb_plane, m0, z_codes[s], z_scales[s]))
+
+        for s in range(2):
+            gather_z(3, s * W, W)
+            interleave_pair(z_grouped[s], 1, z_quad[:, 2:4, cols(s)])
+        gather_z(3, 2 * W, W)
+        interleave_all(z_grouped[2], z_quad[:, :, cols(2)])
+        project_z(0)
+        late_pair = keep.tile([P, 2, W], F32, name="z_grouped0", align_bytes=64)
+        gather(late_pair[:, 0, :], z_windows[2], z_offs, z_gain, 3 * W, W)
+        project_z(1)
+        gather(late_pair[:, 1, :], z_windows[3], z_offs, z_gain, 3 * W, W)
+        interleave_pair(z_grouped[3], 1, late_pair[:])
+        finish(0, 0, 2)
+        finish(0, 2, 2)
+        project_z(2)
+        finish(1, 0, 2)
+        finish(1, 2, 2)
+        project_z(3)
+        finish(2, 0, 2)
+        finish(2, 2, 2)
+        finish(3, 0, 2)
+        finish(3, 2, 1)
+        finish(3, 3, 1)

@@ -1,7 +1,6 @@
 from contextlib import ExitStack
 
 import concourse.mybir as mybir
-from concourse.masks import make_identity
 
 K, N, T, J = 512, 512, 2048, 1024
 FLOPS = 2 * 2 * K * N * J
@@ -15,17 +14,17 @@ U8 = mybir.dt.uint8
 FP8X4 = mybir.dt.float8_e4m3fn_x4
 MULT = mybir.AluOpType.mult
 SILU = mybir.ActivationFunctionType.Silu
+COPY = mybir.ActivationFunctionType.Copy
 
 P = 128
 PACK = 4
 LIST = 16
-HEADS = P // LIST
-CHUNKS = J // P
 M_TILES = N // P
 BANK = 512
 W = 256
 SLICES = J // W
 HALF = J // 2
+EARLY = J - W
 PER_BANK = BANK // W
 
 
@@ -35,7 +34,6 @@ def tile_list_glu_silu_kernel(
     nc = tc.nc
     with ExitStack() as ctx:
         keep = ctx.enter_context(tc.tile_pool(name="keep", bufs=1))
-        ring = ctx.enter_context(tc.tile_pool(name="ring", bufs=2))
         psum = ctx.enter_context(tc.psum_pool(name="psum", bufs=8))
 
         x_offs = keep.tile([P, J // LIST], U16, name="x_offs")
@@ -45,33 +43,34 @@ def tile_list_glu_silu_kernel(
         x_quad = keep.tile([P, PACK, J], F32, name="x_quad")
         z_quad = keep.tile([P, PACK, J], F32, name="z_quad")
         wa_codes = keep.tile([P, N], U32, name="wa_codes", align_bytes=64)
+        wb_codes = keep.tile([P, N], U32, name="wb_codes", align_bytes=64)
         wa_plane = keep.tile([P, N], U8, name="wa_plane", align_bytes=64)
         wb_plane = keep.tile([P, N], U8, name="wb_plane", align_bytes=64)
-        gain_rows = keep.tile([P, P], F32, name="gain_rows")
-        identity = keep.tile([P, P], F32, name="identity")
-        warm = keep.tile([P, 8], F32, name="warm")
-        warm_out = keep.tile([P, 8], F32, name="warm_out")
-        gates = [keep.tile([P, M_TILES, W], F32, name="gate%d" % s) for s in range(SLICES)]
+        bias = keep.tile([P, M_TILES], F32, name="bias")
+        gates = [keep.tile([P, 2, M_TILES, W], F32, name="gate%d" % h) for h in range(2)]
 
-        def stage_tiles(name):
-            grouped = [keep.tile([P, W, PACK], BF16, name="%s_grouped%d" % (name, s), align_bytes=64) for s in range(SLICES)]
-            codes = [keep.tile([P, W], U32, name="%s_codes%d" % (name, s), align_bytes=64) for s in range(SLICES)]
-            planes = [keep.tile([P, W], U8, name="%s_scales%d" % (name, s), align_bytes=64) for s in range(SLICES)]
+        def stage_tiles(name, width):
+            count = J // width
+            grouped = [keep.tile([P, width, PACK], BF16, name="%s_grouped%d" % (name, s), align_bytes=64) for s in range(count)]
+            codes = [keep.tile([P, width], U32, name="%s_codes%d" % (name, s), align_bytes=64) for s in range(count)]
+            planes = [keep.tile([P, width], U8, name="%s_scales%d" % (name, s), align_bytes=64) for s in range(count)]
             return grouped, codes, planes
 
-        x_grouped, x_codes, x_scales = stage_tiles("x")
-        z_grouped, z_codes, z_scales = stage_tiles("z")
+        x_grouped, x_codes, x_scales = stage_tiles("x", HALF)
+        z_grouped, z_codes, z_scales = stage_tiles("z", W)
 
-        make_identity(nc, identity[:])
+        warm = keep.tile([P, 8], F32, name="warm")
+        warm_out = keep.tile([P, 8], F32, name="warm_out")
         nc.vector.memset(warm[:], 0.0)
         nc.scalar.activation(warm_out[:], warm[:], SILU)
+
         nc.vector.memset(wa_plane[:].bitcast(I32), 0)
         nc.vector.memset(wb_plane[:].bitcast(I32), 0)
 
         out_rows = out.rearrange("(m p) j -> p m j", p=P)
 
-        def load_window(source, i):
-            window = keep.tile([P, T], F32, name="window%d" % i)
+        def load_window(name, source, i):
+            window = keep.tile([P, T], F32, name="%s_window%d" % (name, i))
             nc.sync.dma_start(window[:], source.rearrange("(p i) t -> p i t", i=PACK)[:, i, :])
             return window
 
@@ -86,8 +85,8 @@ def tile_list_glu_silu_kernel(
             picked = window[:].indirect(offsets[:, j0 // LIST : (j0 + width) // LIST])
             nc.vector.tensor_tensor(target, picked, gain[:, j0 : j0 + width], MULT)
 
-        def interleave_pair(grouped, u, pair):
-            nc.scalar.copy(grouped[:, :, 2 * u : 2 * u + 2], pair.rearrange("p e j -> p j e"))
+        def interleave_pair(grouped, i0, pair):
+            nc.scalar.copy(grouped[:, :, i0 : i0 + 2], pair.rearrange("p e j -> p j e"))
 
         def interleave_all(grouped, quad):
             nc.scalar.copy(
@@ -98,55 +97,34 @@ def tile_list_glu_silu_kernel(
         def quantize(codes, plane, grouped):
             nc.vector.quantize_mx(out=codes[:].bitcast(FP8X4), scales=plane[:], in_=grouped[:].rearrange("p j i -> p (j i)"))
 
-        def project_bank(w_codes, w_plane, m0, codes, plane):
-            acc = psum.tile([P, PER_BANK, W], F32, name="acc")
-            for m in range(PER_BANK):
-                cols = slice((m0 + m) * P, (m0 + m + 1) * P)
-                nc.tensor.matmul_mx(
-                    out=acc[:, m, :],
-                    lhsT=w_codes[:, cols].bitcast(FP8X4),
-                    lhsT_scale=w_plane[:, cols],
-                    rhs=codes[:].bitcast(FP8X4),
-                    rhs_scale=plane[:],
-                    start=True,
-                    stop=True,
-                )
-            return acc
-
-        for stream, gain_in in enumerate((wgt, wgt2)):
-            nc.sync.dma_start(
-                gain_rows[64 * stream : 64 * (stream + 1), :],
-                gain_in.rearrange("(g r) (c j) -> r g c j", r=LIST, j=P)[0],
+        def project(acc, w_codes, w_plane, m, codes, plane):
+            nc.tensor.matmul_mx(
+                out=acc,
+                lhsT=w_codes[:, m * P : (m + 1) * P].bitcast(FP8X4),
+                lhsT_scale=w_plane[:, m * P : (m + 1) * P],
+                rhs=codes[:].bitcast(FP8X4),
+                rhs_scale=plane[:],
+                start=True,
+                stop=True,
             )
+
         nc.sync.dma_start(x_offs[:], offs)
         nc.sync.dma_start(x_gain[:, :W], wgt[:, :W])
-        x_windows = [load_window(xT, 0), load_window(xT, 1)]
+        x_windows = [load_window("x", xT, 0)]
+        nc.sync.dma_start(x_gain[:, W:], wgt[:, W:])
+        x_windows.append(load_window("x", xT, 1))
         nc.sync.dma_start(z_offs[:], offs2)
-        x_windows.append(load_window(xT, 2))
+        x_windows.append(load_window("x", xT, 2))
         load_scales(wa_plane, wa_scales)
-        x_windows.append(load_window(xT, 3))
+        x_windows.append(load_window("x", xT, 3))
+        nc.sync.dma_start(z_gain[:], wgt2)
+        z_windows = [load_window("z", zT, 0)]
         load_words(wa_codes, wa_words)
         load_scales(wb_plane, wb_scales)
-
-        turned = psum.tile([P, P], F32, name="acc")
-        nc.tensor.transpose(turned[:], gain_rows[:], identity[:])
-        turned_view = turned[:].rearrange("p (s g c) -> p s c g", s=2, g=HEADS)
-
-        def spread_gain(gain, stream, c0, count):
-            spread = ring.tile([P, count, P], F32, name="spread")
-            nc.scalar.copy(
-                spread[:].rearrange("p c (g r) -> p c g r", r=LIST),
-                turned_view[:, stream, c0 : c0 + count, :].unsqueeze(3).to_broadcast([P, count, HEADS, LIST]),
-            )
-            back_turned = psum.tile([P, count, P], F32, name="acc")
-            for c in range(count):
-                nc.tensor.transpose(back_turned[:, c, :], spread[:, c, :], identity[:])
-            nc.scalar.copy(gain[:, c0 * P : (c0 + count) * P].rearrange("p (c j) -> p c j", j=P), back_turned[:])
-
-        spread_gain(x_gain, 0, 2, 2)
-        spread_gain(x_gain, 0, 4, 4)
-        spread_gain(z_gain, 1, 0, 4)
-        spread_gain(z_gain, 1, 4, 4)
+        z_windows.extend(load_window("z", zT, i) for i in range(1, PACK))
+        load_words(wb_codes, wb_words)
+        with nc.allow_non_contiguous_dma(reason="one bias value for each partition and output tile"):
+            nc.sync.dma_start(bias[:], b.rearrange("(m p) -> p m", p=P))
 
         def cols(s):
             return slice(s * W, (s + 1) * W)
@@ -154,73 +132,63 @@ def tile_list_glu_silu_kernel(
         def gather_x(i, j0, width):
             gather(x_quad[:, i, j0 : j0 + width], x_windows[i], x_offs, x_gain, j0, width)
 
-        for j0, width in ((0, W), (W, W), (HALF, HALF)):
-            gather_x(0, j0, width)
-        for h in range(2):
-            gather_x(1, h * HALF, HALF)
-            for s in (2 * h, 2 * h + 1):
-                interleave_pair(x_grouped[s], 0, x_quad[:, 0:2, cols(s)])
-        for h in range(2):
-            gather_x(2, h * HALF, HALF)
-        for s in range(SLICES):
-            gather_x(3, s * W, W)
-            interleave_pair(x_grouped[s], 1, x_quad[:, 2:4, cols(s)])
-
-        z_windows = [load_window(zT, i) for i in range(PACK)]
-
-        for s in range(SLICES):
-            quantize(x_codes[s], x_scales[s], x_grouped[s])
-            for m0 in range(0, M_TILES, PER_BANK):
-                acc = project_bank(wa_codes, wa_plane, m0, x_codes[s], x_scales[s])
-                nc.scalar.activation(gates[s][:, m0 : m0 + PER_BANK, :], acc[:], SILU)
-
-        wb_codes = keep.tile([P, N], U32, name="x_grouped3", align_bytes=64)
-        load_words(wb_codes, wb_words)
-        bias = keep.tile([P, M_TILES], F32, name="x_codes3", align_bytes=64)
-        with nc.allow_non_contiguous_dma(reason="one bias value for each partition and output tile"):
-            nc.sync.dma_start(bias[:], b.rearrange("(m p) -> p m", p=P))
-
         def gather_z(i, j0, width):
             gather(z_quad[:, i, j0 : j0 + width], z_windows[i], z_offs, z_gain, j0, width)
 
+        gather_x(0, 0, W)
+        gather_x(0, W, EARLY)
+        for i in range(1, PACK):
+            for h in range(2):
+                gather_x(i, h * HALF, HALF)
+                if i % 2 == 1:
+                    interleave_pair(x_grouped[h], i - 1, x_quad[:, i - 1 : i + 1, h * HALF : (h + 1) * HALF])
         for h in range(2):
-            gather_z(0, h * HALF, HALF)
-        for h in range(2):
-            gather_z(1, h * HALF, HALF)
+            quantize(x_codes[h], x_scales[h], x_grouped[h])
+            for m in range(M_TILES):
+                acc = psum.tile([P, 2, W], F32, name="acc")
+                project(acc[:].rearrange("p s j -> p (s j)"), wa_codes, wa_plane, m, x_codes[h], x_scales[h])
+                nc.scalar.activation(gates[h][:, :, m, :], acc[:], SILU)
+
+        for i in range(2):
+            for h in range(2):
+                gather_z(i, h * HALF, HALF)
         for s in (0, 1, 3):
             interleave_pair(z_grouped[s], 0, z_quad[:, 0:2, cols(s)])
-        gather_z(2, 0, 3 * W)
-
-        def finish(s, m0, count):
-            acc = banks[(s, m0 - m0 % PER_BANK)]
-            a0 = m0 % PER_BANK
-            product = keep.tile([P, count, W], F32, name="product%d_%d" % (s, m0))
-            result = keep.tile([P, count, W], F32, name="result%d_%d" % (s, m0))
-            nc.vector.tensor_tensor(product[:], acc[:, a0 : a0 + count, :], gates[s][:, m0 : m0 + count, :], MULT)
-            for m in range(count):
-                nc.scalar.activation(result[:, m, :], product[:, m, :], SILU, bias=bias[:, m0 + m : m0 + m + 1])
-            nc.sync.dma_start(out_rows[:, m0 : m0 + count, cols(s)], result[:])
+        gather_z(2, 0, EARLY)
+        gather_z(3, 0, W)
+        interleave_pair(z_grouped[0], 2, z_quad[:, 2:4, cols(0)])
+        gather_z(3, W, HALF)
+        interleave_pair(z_grouped[1], 2, z_quad[:, 2:4, cols(1)])
+        interleave_all(z_grouped[2], z_quad[:, :, cols(2)])
 
         banks = {}
 
         def project_z(s):
             quantize(z_codes[s], z_scales[s], z_grouped[s])
             for m0 in range(0, M_TILES, PER_BANK):
-                banks.setdefault((s, m0), project_bank(wb_codes, wb_plane, m0, z_codes[s], z_scales[s]))
+                acc = psum.tile([P, PER_BANK, W], F32, name="acc")
+                for m in range(PER_BANK):
+                    project(acc[:, m, :], wb_codes, wb_plane, m0 + m, z_codes[s], z_scales[s])
+                banks.setdefault((s, m0), acc)
 
-        for s in range(2):
-            gather_z(3, s * W, W)
-            interleave_pair(z_grouped[s], 1, z_quad[:, 2:4, cols(s)])
-        gather_z(3, 2 * W, W)
-        interleave_all(z_grouped[2], z_quad[:, :, cols(2)])
+        def finish(s, m0, count):
+            acc = banks[(s, m0 - m0 % PER_BANK)]
+            a0 = m0 % PER_BANK
+            product = keep.tile([P, count, W], F32, name="product%d_%d" % (s, m0))
+            result = keep.tile([P, count, W], F32, name="result%d_%d" % (s, m0))
+            nc.vector.tensor_tensor(product[:], acc[:, a0 : a0 + count, :], gates[s // 2][:, s % 2, m0 : m0 + count, :], MULT)
+            for m in range(count):
+                nc.scalar.activation(result[:, m, :], product[:, m, :], SILU, bias=bias[:, m0 + m : m0 + m + 1])
+            nc.sync.dma_start(out_rows[:, m0 : m0 + count, cols(s)], result[:])
+
         project_z(0)
         late_pair = keep.tile([P, 2, W], F32, name="z_grouped0", align_bytes=64)
-        gather(late_pair[:, 0, :], z_windows[2], z_offs, z_gain, 3 * W, W)
+        gather(late_pair[:, 0, :], z_windows[2], z_offs, z_gain, EARLY, W)
         project_z(1)
-        gather(late_pair[:, 1, :], z_windows[3], z_offs, z_gain, 3 * W, W)
-        interleave_pair(z_grouped[3], 1, late_pair[:])
         finish(0, 0, 2)
         finish(0, 2, 2)
+        gather(late_pair[:, 1, :], z_windows[3], z_offs, z_gain, EARLY, W)
+        interleave_pair(z_grouped[3], 2, late_pair[:])
         project_z(2)
         finish(1, 0, 2)
         finish(1, 2, 2)

from contextlib import ExitStack

import concourse.mybir as mybir

K, N, T, J = 512, 512, 2048, 1024
FLOPS = 2 * 2 * K * N * J

F32 = mybir.dt.float32
BF16 = mybir.dt.bfloat16
I32 = mybir.dt.int32
U32 = mybir.dt.uint32
U16 = mybir.dt.uint16
U8 = mybir.dt.uint8
FP8X4 = mybir.dt.float8_e4m3fn_x4
MULT = mybir.AluOpType.mult
SILU = mybir.ActivationFunctionType.Silu
COPY = mybir.ActivationFunctionType.Copy

P = 128
PACK = 4
LIST = 16
M_TILES = N // P
BANK = 512
W = 256
SLICES = J // W
HALF = J // 2
EARLY = J - W
PER_BANK = BANK // W


def tile_list_glu_silu_kernel(
    tc, xT, wgt, zT, wgt2, wa_words, wa_scales, wb_words, wb_scales, b, offs, offs2, out
):
    nc = tc.nc
    with ExitStack() as ctx:
        keep = ctx.enter_context(tc.tile_pool(name="keep", bufs=1))
        psum = ctx.enter_context(tc.psum_pool(name="psum", bufs=8))

        x_offs = keep.tile([P, J // LIST], U16, name="x_offs")
        z_offs = keep.tile([P, J // LIST], U16, name="z_offs")
        x_gain = keep.tile([P, J], F32, name="x_gain")
        z_gain = keep.tile([P, J], F32, name="z_gain")
        x_quad = keep.tile([P, PACK, J], F32, name="x_quad")
        z_quad = keep.tile([P, PACK, J], F32, name="z_quad")
        wa_codes = keep.tile([P, N], U32, name="wa_codes", align_bytes=64)
        wb_codes = keep.tile([P, N], U32, name="wb_codes", align_bytes=64)
        wa_plane = keep.tile([P, N], U8, name="wa_plane", align_bytes=64)
        wb_plane = keep.tile([P, N], U8, name="wb_plane", align_bytes=64)
        bias = keep.tile([P, M_TILES], F32, name="bias")
        gates = [keep.tile([P, 2, M_TILES, W], F32, name="gate%d" % h) for h in range(2)]

        def stage_tiles(name, width):
            count = J // width
            grouped = [keep.tile([P, width, PACK], BF16, name="%s_grouped%d" % (name, s), align_bytes=64) for s in range(count)]
            codes = [keep.tile([P, width], U32, name="%s_codes%d" % (name, s), align_bytes=64) for s in range(count)]
            planes = [keep.tile([P, width], U8, name="%s_scales%d" % (name, s), align_bytes=64) for s in range(count)]
            return grouped, codes, planes

        x_grouped, x_codes, x_scales = stage_tiles("x", HALF)
        z_grouped, z_codes, z_scales = stage_tiles("z", W)

        warm = keep.tile([P, 8], F32, name="warm")
        warm_out = keep.tile([P, 8], F32, name="warm_out")
        nc.vector.memset(warm[:], 0.0)
        nc.scalar.activation(warm_out[:], warm[:], SILU)

        nc.vector.memset(wa_plane[:].bitcast(I32), 0)
        nc.vector.memset(wb_plane[:].bitcast(I32), 0)

        out_rows = out.rearrange("(m p) j -> p m j", p=P)

        def load_window(name, source, i):
            window = keep.tile([P, T], F32, name="%s_window%d" % (name, i))
            nc.sync.dma_start(window[:], source.rearrange("(p i) t -> p i t", i=PACK)[:, i, :])
            return window

        def load_scales(plane, scales):
            for q in range(4):
                nc.sync.dma_start(plane[32 * q : 32 * q + 4, :].bitcast(I32), scales[0, 4 * q : 4 * q + 4, :].bitcast(I32))

        def load_words(codes, words):
            nc.sync.dma_start(codes[:].bitcast(I32), words[0].rearrange("p n i -> p (n i)").bitcast(I32))

        def gather(target, window, offsets, gain, j0, width):
            picked = window[:].indirect(offsets[:, j0 // LIST : (j0 + width) // LIST])
            nc.vector.tensor_tensor(target, picked, gain[:, j0 : j0 + width], MULT)

        def interleave_pair(grouped, i0, pair):
            nc.scalar.copy(grouped[:, :, i0 : i0 + 2], pair.rearrange("p e j -> p j e"))

        def interleave_all(grouped, quad):
            nc.scalar.copy(
                grouped[:].rearrange("p (c r) i -> p c i r", r=4),
                quad.rearrange("p i (c r) -> p c i r", r=4),
            )

        def quantize(codes, plane, grouped):
            nc.vector.quantize_mx(out=codes[:].bitcast(FP8X4), scales=plane[:], in_=grouped[:].rearrange("p j i -> p (j i)"))

        def project(acc, w_codes, w_plane, m, codes, plane):
            nc.tensor.matmul_mx(
                out=acc,
                lhsT=w_codes[:, m * P : (m + 1) * P].bitcast(FP8X4),
                lhsT_scale=w_plane[:, m * P : (m + 1) * P],
                rhs=codes[:].bitcast(FP8X4),
                rhs_scale=plane[:],
                start=True,
                stop=True,
            )

        nc.sync.dma_start(x_offs[:], offs)
        nc.sync.dma_start(x_gain[:, :W], wgt[:, :W])
        x_windows = [load_window("x", xT, 0)]
        nc.sync.dma_start(x_gain[:, W:], wgt[:, W:])
        x_windows.append(load_window("x", xT, 1))
        nc.sync.dma_start(z_offs[:], offs2)
        x_windows.append(load_window("x", xT, 2))
        load_scales(wa_plane, wa_scales)
        x_windows.append(load_window("x", xT, 3))
        nc.sync.dma_start(z_gain[:], wgt2)
        z_windows = [load_window("z", zT, 0)]
        load_words(wa_codes, wa_words)
        load_scales(wb_plane, wb_scales)
        z_windows.extend(load_window("z", zT, i) for i in range(1, PACK))
        load_words(wb_codes, wb_words)
        with nc.allow_non_contiguous_dma(reason="one bias value for each partition and output tile"):
            nc.sync.dma_start(bias[:], b.rearrange("(m p) -> p m", p=P))

        def cols(s):
            return slice(s * W, (s + 1) * W)

        def gather_x(i, j0, width):
            gather(x_quad[:, i, j0 : j0 + width], x_windows[i], x_offs, x_gain, j0, width)

        def gather_z(i, j0, width):
            gather(z_quad[:, i, j0 : j0 + width], z_windows[i], z_offs, z_gain, j0, width)

        gather_x(0, 0, W)
        gather_x(0, W, EARLY)
        for i in range(1, PACK):
            for h in range(2):
                gather_x(i, h * HALF, HALF)
                if i % 2 == 1:
                    interleave_pair(x_grouped[h], i - 1, x_quad[:, i - 1 : i + 1, h * HALF : (h + 1) * HALF])
        for h in range(2):
            quantize(x_codes[h], x_scales[h], x_grouped[h])
            for m in range(M_TILES):
                acc = psum.tile([P, 2, W], F32, name="acc")
                project(acc[:].rearrange("p s j -> p (s j)"), wa_codes, wa_plane, m, x_codes[h], x_scales[h])
                nc.scalar.activation(gates[h][:, :, m, :], acc[:], SILU)

        for i in range(2):
            for h in range(2):
                gather_z(i, h * HALF, HALF)
        for s in (0, 1, 3):
            interleave_pair(z_grouped[s], 0, z_quad[:, 0:2, cols(s)])
        gather_z(2, 0, EARLY)
        gather_z(3, 0, W)
        interleave_pair(z_grouped[0], 2, z_quad[:, 2:4, cols(0)])
        gather_z(3, W, HALF)
        interleave_pair(z_grouped[1], 2, z_quad[:, 2:4, cols(1)])
        interleave_all(z_grouped[2], z_quad[:, :, cols(2)])

        banks = {}

        def project_z(s):
            quantize(z_codes[s], z_scales[s], z_grouped[s])
            for m0 in range(0, M_TILES, PER_BANK):
                acc = psum.tile([P, PER_BANK, W], F32, name="acc")
                for m in range(PER_BANK):
                    project(acc[:, m, :], wb_codes, wb_plane, m0 + m, z_codes[s], z_scales[s])
                banks.setdefault((s, m0), acc)

        def finish(s, m0, count):
            acc = banks[(s, m0 - m0 % PER_BANK)]
            a0 = m0 % PER_BANK
            product = keep.tile([P, count, W], F32, name="product%d_%d" % (s, m0))
            result = keep.tile([P, count, W], F32, name="result%d_%d" % (s, m0))
            nc.vector.tensor_tensor(product[:], acc[:, a0 : a0 + count, :], gates[s // 2][:, s % 2, m0 : m0 + count, :], MULT)
            for m in range(count):
                nc.scalar.activation(result[:, m, :], product[:, m, :], SILU, bias=bias[:, m0 + m : m0 + m + 1])
            nc.sync.dma_start(out_rows[:, m0 : m0 + count, cols(s)], result[:])

        project_z(0)
        late_pair = keep.tile([P, 2, W], F32, name="z_grouped0", align_bytes=64)
        gather(late_pair[:, 0, :], z_windows[2], z_offs, z_gain, EARLY, W)
        project_z(1)
        finish(0, 0, 2)
        finish(0, 2, 2)
        gather(late_pair[:, 1, :], z_windows[3], z_offs, z_gain, EARLY, W)
        interleave_pair(z_grouped[3], 2, late_pair[:])
        project_z(2)
        finish(1, 0, 2)
        finish(1, 2, 2)
        project_z(3)
        finish(2, 0, 2)
        finish(2, 2, 2)
        finish(3, 0, 2)
        finish(3, 2, 1)
        finish(3, 3, 1)
